import numpy as np
import ml_dtypes


def mxq(x, axis, fmt="e4m3"):
    dtype, down = {"e4m3": (ml_dtypes.float8_e4m3fn, 7), "e5m2": (ml_dtypes.float8_e5m2, 14)}[fmt]
    v = np.moveaxis(np.asarray(x, np.float32).astype(ml_dtypes.bfloat16).astype(np.float64), axis, -1)
    blocks = v.reshape(v.shape[:-1] + (-1, 32))
    amax = np.abs(blocks).max(-1, keepdims=True)
    byte = np.maximum(np.where(amax > 0, np.frexp(amax)[1] - 1 + 127, 0) - down, 1)
    scale = np.exp2(byte - 127.0)
    codes = (blocks / scale).astype(np.float32).astype(dtype).astype(np.float64)
    return np.moveaxis((codes * scale).reshape(v.shape), -1, axis)


WIDE = False


def mx_kscale(k):
    if not WIDE:
        return np.ones(k)
    levels = np.array([10, -10, 5, -5, 0])
    if k % 512:
        return np.exp2(np.random.permutation(np.resize(levels, k // 32))).repeat(32)
    a = np.empty((k // 512, 16))
    for p in range(k // 512):
        a[p, :8] = np.random.permutation(np.resize(levels, 8))
        for g in range(8):
            far = levels[np.abs(levels - a[p, g]) >= 10]
            a[p, g + 8] = far[np.random.randint(len(far))]
    return np.exp2(a.ravel()).repeat(32)


def f64(x):
    return np.asarray(x).astype(np.float64)


def striped(idx):
    return np.tile(idx.reshape(-1, 16).T, (8, 1)).astype(np.uint16)


def unstriped(offs):
    return offs[:16].T.reshape(-1).astype(np.int64)


E2M1 = np.array([0.0, 0.5, 1.0, 1.5, 2.0, 3.0, 4.0, 6.0, -0.0, -0.5, -1.0, -1.5, -2.0, -3.0, -4.0, -6.0])


def pack_weight(w, fmt):
    k, n = w.shape
    w = f64(np.asarray(w, np.float32).astype(ml_dtypes.bfloat16)).reshape(k // 32, 32, n)
    amax = np.abs(w).max(1)
    if fmt == "e4m3":
        byte = np.frexp(amax)[1] - 1 + 127 - 7
    else:
        mant, ex = np.frexp(amax / 6.0)
        byte = np.where(mant > 0.5, ex, ex - 1) + 127
    byte = np.clip(np.where(amax > 0, byte, 1), 1, 254)
    scaled = (w * np.exp2(127.0 - byte)[:, None, :]).reshape(k, n).astype(np.float32)
    by_word = np.ascontiguousarray(scaled.reshape(k // 512, 128, 4, n).transpose(0, 1, 3, 2))
    if fmt == "e4m3":
        words = by_word.astype(ml_dtypes.float8_e4m3fn).view(np.uint8)
    else:
        c = by_word.astype(ml_dtypes.float4_e2m1fn).view(np.uint8) & 0xF
        words = (c[..., 0::2] | (c[..., 1::2] << 4)).reshape(k // 512, 128, 2 * n)
    return np.ascontiguousarray(words), np.ascontiguousarray(byte.astype(np.uint8).reshape(k // 512, 16, n))


def unpack_weight(words, scales, fmt):
    g, _, n = scales.shape
    words = np.ascontiguousarray(words).reshape(g, 128, n, -1)
    if fmt == "e4m3":
        vals = words.view(ml_dtypes.float8_e4m3fn).astype(np.float64)
    else:
        nib = np.empty((g, 128, n, 4), np.uint8)
        nib[..., 0::2] = words & 0xF
        nib[..., 1::2] = words >> 4
        vals = E2M1[nib]
    vals = vals * np.repeat(np.exp2(scales.astype(np.float64) - 127.0), 8, axis=1)[..., None]
    return vals.transpose(0, 1, 3, 2).reshape(g * 512, n)


def gelu(v):
    return 0.5 * v * (1.0 + np.tanh(np.sqrt(2.0 / np.pi) * (v + 0.044715 * v**3)))


def bf(x):
    return np.asarray(x, np.float32).astype(ml_dtypes.bfloat16)

def planes(Y):
    n, m = Y.shape
    b = f64(bf(Y)).reshape(n // 32, 32, m)
    amax = np.abs(b).max(1)
    byte = np.clip(np.where(amax > 0, np.frexp(amax)[1] - 1 + 127 - 7, 1), 1, 254)
    codes = (b * np.exp2(127.0 - byte)[:, None, :]).reshape(n, m).astype(np.float32).astype(ml_dtypes.float8_e4m3fn).view(np.uint8)
    words = codes.reshape(n // 512, 128, 4, m).transpose(0, 1, 3, 2)
    return np.ascontiguousarray(words), np.ascontiguousarray(byte.astype(np.uint8).reshape(n // 512, 16, m))


K, H, N, T, S, T2, P = 1024, 1536, 1024, 2048, 512, 2048, 128

def setup_inputs():
    n = np.random.standard_normal
    s = mx_kscale(K)[:, None]
    u = mx_kscale(H)[:, None]
    tab_words, tab_scales = pack_weight(n((K, T)) * s, "e4m3")
    wk = n((K, H)) / np.sqrt(K) / s * np.sqrt(u).T
    wk_words, wk_scales = pack_weight(wk, "e2m1")
    wr = n((K, N)) / np.sqrt(K) / s
    wv = n((H, N)) / np.sqrt(H) / u * np.exp(0.8 * n(N))[None, :]
    wv_words, wv_scales = pack_weight(wv, "e4m3")
    return {
        "tab_words": tab_words, "tab_scales": tab_scales,
        "offs": striped(np.random.permutation(T)[:S]),
        "wk_words": wk_words, "wk_scales": wk_scales,
        "wr": wr.astype(np.float32),
        "wv_words": wv_words, "wv_scales": wv_scales,
        "wgo": np.exp(0.3 * n((P, S))).astype(np.float32),
        "offs2": striped(np.random.permutation(T2)[:S]),
    }

def reference(tab_words, tab_scales, offs, wk_words, wk_scales, wr, wv_words, wv_scales, wgo, offs2):
    v = unpack_weight(tab_words, tab_scales, "e4m3")[:, unstriped(offs)]
    wk = unpack_weight(wk_words, wk_scales, "e2m1")
    wv = unpack_weight(wv_words, wv_scales, "e4m3")
    key = wk.T @ v
    h = np.square(np.maximum(key, 0.0))
    rec = mxq(f64(wr), 0, "e4m3").T @ v
    val = wv.T @ mxq(h, 0, "e4m3")
    y = val * (1.0 / (1.0 + np.exp(-rec)))
    page = np.zeros((N, T2))
    page[:, unstriped(offs2)] = np.tile(f64(wgo), (N // P, 1)) * y
    y = page
    words, scales = planes(y)
    return y, words, scales

@@ -1,0 +1,349 @@
+from contextlib import ExitStack
+
+import concourse.mybir as mybir
+
+K, H, N, T, S, T2 = 1024, 1536, 1024, 2048, 512, 2048
+FLOPS = 2 * S * (K * H + K * N + H * N)
+
+F32 = mybir.dt.float32
+BF16 = mybir.dt.bfloat16
+I32 = mybir.dt.int32
+U32 = mybir.dt.uint32
+U16 = mybir.dt.uint16
+U8 = mybir.dt.uint8
+FP8X4 = mybir.dt.float8_e4m3fn_x4
+FP4X4 = mybir.dt.float4_e2m1fn_x4
+ACT = mybir.ActivationFunctionType
+ALU = mybir.AluOpType
+
+P = 128
+PACK = 4
+PASS = P * PACK
+QUADS = 4
+K_PASSES, H_PASSES, N_GROUPS = K // PASS, H // PASS, N // PASS
+CHUNK = 512
+CHUNKS = T2 // CHUNK
+PAGES = 4
+RELU_ON_SCALAR = 7
+TAIL_CHUNKS_ON_VECTOR = 2
+
+
+def tile_list_rwkv_channel_mix_kernel(
+    tc, tab_words, tab_scales, offs, wk_words, wk_scales, wr, wv_words, wv_scales, wgo, offs2, out_0, out_1, out_2
+):
+    nc = tc.nc
+    with ExitStack() as ctx:
+        lists = ctx.enter_context(tc.tile_pool(name="lists", bufs=1))
+        pool = ctx.enter_context(tc.tile_pool(name="sbuf", bufs=1))
+        psum = ctx.enter_context(tc.psum_pool(name="psum", bufs=8))
+
+        def held(name, width, dtype, tag=None, bufs=1):
+            return pool.tile([P, width], dtype, name=name, tag=tag or name, bufs=bufs, align_bytes=64)
+
+        def bank(name):
+            return psum.tile([P, S], F32, name=name, tag="bank")
+
+        picks = lists.tile([P, S // 16], U16, name="picks")
+        places = lists.tile([P, S // 16], U16, name="places")
+        nc.sync.dma_start(picks[:], offs)
+
+        wk_raw = held("wk_raw", K_PASSES * 2 * H, U8, tag="weight_raw")
+        nc.sync.dma_start(
+            wk_raw[:].bitcast(I32).rearrange("p (a w) -> p a w", a=K_PASSES),
+            wk_words.bitcast(I32).rearrange("a p w -> p a w"),
+        )
+        tab = [held(f"tab{a}", T, I32, tag=f"pass_raw{a}") for a in range(K_PASSES)]
+        for a in range(K_PASSES):
+            nc.sync.dma_start(tab[a][:], tab_words[a].rearrange("p t i -> p (t i)").bitcast(I32))
+        nc.sync.dma_start(places[:], offs2)
+
+        tab_sc = held("tab_sc", K_PASSES * T, U8)
+        wk_sc_raw = held("wk_sc_raw", K_PASSES * H, U8, tag="wk_sc_then_wgo")
+        wv_sc_raw = held("wv_sc_raw", N, U8)
+        for plane in (wk_sc_raw, tab_sc, wv_sc_raw):
+            nc.vector.memset(plane[:].bitcast(I32), 0)
+        for q in range(QUADS):
+            nc.scalar.dma_start(
+                tab_sc[32 * q : 32 * q + 4, :].bitcast(I32).rearrange("r (a w) -> r a w", a=K_PASSES),
+                tab_scales[:, 4 * q : 4 * q + 4, :].bitcast(I32).rearrange("a r w -> r a w"),
+            )
+        for q in range(QUADS):
+            nc.gpsimd.dma_start(
+                wk_sc_raw[32 * q : 32 * q + 4, :].bitcast(I32).rearrange("r (a w) -> r a w", a=K_PASSES),
+                wk_scales[:, 4 * q : 4 * q + 4, :].bitcast(I32).rearrange("a r w -> r a w"),
+            )
+        for q in range(QUADS):
+            nc.gpsimd.dma_start(
+                wv_sc_raw[32 * q : 32 * q + 4 * H_PASSES, :].bitcast(I32),
+                wv_scales[:, 4 * q : 4 * q + 4, :].bitcast(I32),
+            )
+
+        pages = [held("page0", T2, F32), held("page1", T2, F32)]
+        for page in pages:
+            nc.vector.memset(page[:, : T2 // 2 - 1], 0.0)
+            nc.vector.memset(page[:, T2 // 2 - 1 :], 0.0)
+
+        wk_codes = [held(f"wk_codes{b}", K_PASSES * 2 * PASS, U8) for b in range(H_PASSES)]
+        wk_sc = [held(f"wk_sc{b}", K_PASSES * PASS, U8) for b in range(H_PASSES)]
+        v_codes = [held(f"v_codes{a}", S, U32) for a in range(K_PASSES)]
+        v_sc = [held(f"v_sc{a}", S, U8) for a in range(K_PASSES)]
+
+        def deal_wk_codes(b):
+            nc.scalar.copy(
+                wk_codes[b][:].bitcast(U16).rearrange("p (a t q) -> p a q t", a=K_PASSES, t=PACK),
+                wk_raw[:].bitcast(U16).rearrange("p (a b q t) -> p b a q t", a=K_PASSES, b=H_PASSES, t=PACK)[:, b],
+            )
+
+        def deal_wk_scales(b):
+            nc.vector.tensor_copy(
+                wk_sc[b][:].rearrange("p (a t q) -> p a q t", a=K_PASSES, t=PACK),
+                wk_sc_raw[:].rearrange("p (a b q t) -> p b a q t", a=K_PASSES, b=H_PASSES, t=PACK)[:, b],
+            )
+
+        def gather_codes(a):
+            nc.vector.tensor_copy(v_codes[a][:], tab[a][:].bitcast(U32).indirect(picks[:]))
+
+        def gather_scales(a):
+            nc.vector.tensor_copy(v_sc[a][:], tab_sc[:, a * T : (a + 1) * T].indirect(picks[:]))
+
+        for b in range(H_PASSES):
+            deal_wk_codes(b)
+        gather_scales(0)
+        gather_codes(0)
+        deal_wk_scales(0)
+        gather_scales(1)
+        gather_codes(1)
+        for b in range(1, H_PASSES):
+            deal_wk_scales(b)
+
+        wr_codes = {}
+        wr_sc = {}
+        wr_raw = {}
+        wv_raw = {}
+        wv_codes = {}
+
+        def load_wr(a, g):
+            wr_raw[a, g] = held(f"wr_raw{a}{g}", PACK * PASS, F32, tag=f"pass_raw{a}")
+            nc.sync.dma_start(
+                wr_raw[a, g][:].rearrange("p (j w) -> p j w", j=PACK),
+                wr[a * PASS : (a + 1) * PASS, g * PASS : (g + 1) * PASS].rearrange("(p j) w -> p j w", j=PACK),
+            )
+
+        def quantize_wr(a, g, on_scalar):
+            rounded = held(f"wr_bf{a}{g}", PACK * PASS, BF16, tag="wr_bf", bufs=2)
+            dst = rounded[:].rearrange("p (t m j) -> p m j t", t=PACK, j=PACK)
+            src = wr_raw[a, g][:].rearrange("p (j m t) -> p m j t", j=PACK, t=PACK)
+            if on_scalar:
+                nc.scalar.copy(dst, src)
+            else:
+                nc.vector.tensor_copy(dst, src)
+            wr_codes[a, g] = held(f"wr_codes{a}{g}", PASS, U32)
+            wr_sc[a, g] = held(f"wr_sc{a}{g}", PASS, U8)
+            nc.vector.quantize_mx(out=wr_codes[a, g][:].bitcast(FP8X4), scales=wr_sc[a, g][:], in_=rounded[:])
+
+        def load_wv(g):
+            wv_raw[g] = held(f"wv_raw{g}", H_PASSES * PASS, I32, tag="weight_raw")
+            nc.sync.dma_start(
+                wv_raw[g][:].rearrange("p (b w) -> p b w", b=H_PASSES),
+                wv_words[:, :, g * PASS : (g + 1) * PASS, :]
+                .rearrange("b p n i -> b p (n i)")
+                .bitcast(I32)
+                .rearrange("b p w -> p b w"),
+            )
+
+        def deal_wv_codes(g):
+            wv_codes[g] = held(f"wv_codes{g}", H_PASSES * PASS, I32)
+            nc.vector.tensor_copy(
+                wv_codes[g][:].rearrange("p (b t q) -> p b q t", b=H_PASSES, t=PACK),
+                wv_raw[g][:].rearrange("p (b q t) -> p b q t", b=H_PASSES, t=PACK),
+            )
+
+        load_wr(0, 0)
+        load_wv(0)
+        load_wr(1, 0)
+        gains = held("gains", PACK * S, F32, tag="wk_sc_then_wgo")
+        for q in range(QUADS):
+            nc.sync.dma_start(gains[32 * q : 32 * q + 32, :], wgo.rearrange("(p t) j -> p (t j)", t=PACK))
+
+        h_codes = [held(f"h_codes{b}", S, U32) for b in range(H_PASSES)]
+        h_sc = [held(f"h_sc{b}", S, U8) for b in range(H_PASSES)]
+
+        def key_group(b):
+            relu = held(f"relu{b}", PACK * S, F32, tag="relu", bufs=2)
+            for t in range(PACK):
+                acc = bank(f"key{b}{t}")
+                for a in range(K_PASSES):
+                    col = a * PASS + t * P
+                    nc.tensor.matmul_mx(
+                        out=acc[:],
+                        lhsT=wk_codes[b][:, 2 * col : 2 * (col + P)].bitcast(FP4X4),
+                        lhsT_scale=wk_sc[b][:, col : col + P],
+                        rhs=v_codes[a][:].bitcast(FP8X4),
+                        rhs_scale=v_sc[a][:],
+                        start=(a == 0),
+                        stop=(a == K_PASSES - 1),
+                    )
+                dst = relu[:, t * S : (t + 1) * S]
+                if PACK * b + t < RELU_ON_SCALAR:
+                    nc.scalar.activation(dst, acc[:], ACT.Relu)
+                else:
+                    nc.vector.tensor_scalar_max(dst, acc[:], 0.0)
+            return relu
+
+        def square_group(b, relu):
+            h_bf = held(f"h_bf{b}", PACK * S, BF16)
+            src = relu[:].rearrange("p (t c i) -> p c t i", t=PACK, i=4)
+            dst = h_bf[:].rearrange("p (c i t) -> p c t i", t=PACK, i=4)
+            if b < H_PASSES - 1:
+                nc.scalar.activation(dst, src, ACT.Square)
+            else:
+                half = S // 4 // 2
+                nc.scalar.activation(dst[:, :half], src[:, :half], ACT.Square)
+                nc.vector.tensor_tensor(dst[:, half:], src[:, half:], src[:, half:], ALU.mult)
+            return h_bf
+
+        def quantize_h(b, h_bf):
+            nc.vector.quantize_mx(out=h_codes[b][:].bitcast(FP8X4), scales=h_sc[b][:], in_=h_bf[:])
+
+        gates = {}
+
+        def gate(i):
+            g, t = divmod(i, PACK)
+            acc = bank(f"rec{i}")
+            for a in range(K_PASSES):
+                nc.tensor.matmul_mx(
+                    out=acc[:],
+                    lhsT=wr_codes[a, g][:, t * P : (t + 1) * P].bitcast(FP8X4),
+                    lhsT_scale=wr_sc[a, g][:, t * P : (t + 1) * P],
+                    rhs=v_codes[a][:].bitcast(FP8X4),
+                    rhs_scale=v_sc[a][:],
+                    start=(a == 0),
+                    stop=(a == K_PASSES - 1),
+                )
+            if i == 0:
+                gates[i] = held("gate0", S, F32, tag="gate0_then_page")
+            else:
+                gates[i] = held(f"gate{i}", S, F32, tag="gate", bufs=3)
+            nc.scalar.activation(gates[i][:], acc[:], ACT.Sigmoid)
+
+        relu0 = key_group(0)
+        quantize_wr(0, 0, False)
+        h_bf0 = square_group(0, relu0)
+        deal_wv_codes(0)
+        wv_sc = held("wv_sc", N, U8)
+        nc.vector.tensor_copy(
+            wv_sc[:].rearrange("p (g t q) -> p g q t", g=N_GROUPS, t=PACK),
+            wv_sc_raw[:].rearrange("p (g q t) -> p g q t", g=N_GROUPS, t=PACK),
+        )
+        load_wv(1)
+        load_wr(0, 1)
+        relu1 = key_group(1)
+        quantize_h(0, h_bf0)
+        quantize_wr(1, 0, False)
+        load_wr(1, 1)
+        h_bf1 = square_group(1, relu1)
+        relu2 = key_group(2)
+        gate(0)
+        quantize_h(1, h_bf1)
+        h_bf2 = square_group(2, relu2)
+        quantize_h(2, h_bf2)
+        pages.append(held("page2", T2, F32, tag="h_bf2"))
+        nc.gpsimd.memset(pages[2][:], 0.0)
+
+        gated = {}
+
+        def value(i):
+            g, t = divmod(i, PACK)
+            acc = bank(f"val{i}")
+            for b in range(H_PASSES):
+                col = b * PASS + t * P
+                nc.tensor.matmul_mx(
+                    out=acc[:],
+                    lhsT=wv_codes[g][:, col : col + P].bitcast(FP8X4),
+                    lhsT_scale=wv_sc[4 * b :, g * PASS + t * P : g * PASS + (t + 1) * P],
+                    rhs=h_codes[b][:].bitcast(FP8X4),
+                    rhs_scale=h_sc[b][:],
+                    start=(b == 0),
+                    stop=(b == H_PASSES - 1),
+                )
+            gated[i] = held(f"gated{i}", S, F32, tag="gated", bufs=3)
+            nc.vector.tensor_tensor(gated[i][:], acc[:], gates[i][:], ALU.mult)
+
+        out_rows = out_0.rearrange("(g p t) m -> g t p m", t=PACK, p=P)
+
+        def scatter(i):
+            g, t = divmod(i, PACK)
+            page = pages[i % PAGES]
+            nc.vector.tensor_tensor(
+                page[:].indirect(places[:]), gated[i][:], gains[:, t * S : (t + 1) * S], ALU.mult
+            )
+            nc.sync.dma_start(out_rows[g, t], page[:])
+
+        pairs = {}
+
+        def on_vector(i, c):
+            return i >= N_GROUPS * PACK - 2 and c < TAIL_CHUNKS_ON_VECTOR
+
+        def round_page(i, c):
+            g, t = divmod(i, PACK)
+            if t == 0:
+                pairs[g, c] = held(f"pairs{g}{c}", PACK * CHUNK, BF16, tag=f"pairs{c}")
+            dst = pairs[g, c][:].rearrange("p (u m e) -> p u m e", u=2, e=2)[:, t // 2, :, t % 2]
+            src = pages[i % PAGES][:, c * CHUNK : (c + 1) * CHUNK]
+            if on_vector(i, c):
+                nc.vector.tensor_copy(dst, src)
+            else:
+                nc.scalar.copy(dst, src)
+
+        y_sc = {}
+
+        def planes(g, c):
+            woven = held(f"woven{g}{c}", PACK * CHUNK, BF16, tag="woven", bufs=3)
+            if on_vector(PACK * g + PACK - 1, c):
+                nc.vector.tensor_copy(
+                    woven[:].bitcast(I32).rearrange("p (m u) -> p m u", u=2),
+                    pairs[g, c][:].bitcast(I32).rearrange("p (u m) -> p m u", u=2),
+                )
+            else:
+                nc.scalar.copy(
+                    woven[:].bitcast(U32).rearrange("p (m u) -> p m u", u=2),
+                    pairs[g, c][:].bitcast(U32).rearrange("p (u m) -> p m u", u=2),
+                )
+            if c == 0:
+                y_sc[g] = held(f"y_sc{g}", CHUNK, U8)
+            codes = held(f"y_codes{g}{c}", CHUNK, I32, tag="y_codes", bufs=4)
+            nc.vector.quantize_mx(out=codes[:].bitcast(FP8X4), scales=y_sc[g][4 * c :, :], in_=woven[:])
+            nc.sync.dma_start(
+                out_1[g].rearrange("p m t -> p (m t)").bitcast(I32)[:, c * CHUNK : (c + 1) * CHUNK], codes[:]
+            )
+
+        def store_scales(g, queue):
+            for q in range(QUADS):
+                queue.dma_start(
+                    out_2[g, 4 * q : 4 * q + 4, :].bitcast(I32).rearrange("r (c w) -> c r w", c=CHUNKS),
+                    y_sc[g][32 * q : 32 * q + 4 * CHUNKS, :].bitcast(I32),
+                )
+
+        last = N_GROUPS * PACK - 1
+        value(0)
+        gate(1)
+        pages.append(held("page3", T2, F32, tag="gate0_then_page"))
+        nc.gpsimd.memset(pages[3][:], 0.0)
+        for i in range(last + 1):
+            if i < last:
+                value(i + 1)
+            if i + 2 <= last:
+                gate(i + 2)
+            scatter(i)
+            if i == 0:
+                quantize_wr(0, 1, True)
+                deal_wv_codes(1)
+            if i == 1:
+                quantize_wr(1, 1, False)
+            for c in range(CHUNKS):
+                round_page(i, c)
+                if i % PACK == PACK - 1:
+                    planes(i // PACK, c)
+            if i == PACK - 1:
+                store_scales(0, nc.sync)
+        store_scales(1, nc.scalar)

@@ -24,8 +24,9 @@ K_PASSES, H_PASSES, N_GROUPS = K // PASS, H // PASS, N // PASS
 CHUNK = 512
 CHUNKS = T2 // CHUNK
 PAGES = 4
-RELU_ON_SCALAR = 7
-TAIL_CHUNKS_ON_VECTOR = 2
+HALVES = 2
+HALF = S // HALVES
+PAIRS = PACK // 2
 
 
 def tile_list_rwkv_channel_mix_kernel(
@@ -35,53 +36,44 @@ def tile_list_rwkv_channel_mix_kernel(
     with ExitStack() as ctx:
         lists = ctx.enter_context(tc.tile_pool(name="lists", bufs=1))
         pool = ctx.enter_context(tc.tile_pool(name="sbuf", bufs=1))
-        psum = ctx.enter_context(tc.psum_pool(name="psum", bufs=8))
+        psum = ctx.enter_context(tc.psum_pool(name="psum", bufs=1))
 
         def held(name, width, dtype, tag=None, bufs=1):
             return pool.tile([P, width], dtype, name=name, tag=tag or name, bufs=bufs, align_bytes=64)
 
-        def bank(name):
-            return psum.tile([P, S], F32, name=name, tag="bank")
+        def bank(name, tag, bufs):
+            return psum.tile([P, S], F32, name=name, tag=tag, bufs=bufs)
 
         picks = lists.tile([P, S // 16], U16, name="picks")
         places = lists.tile([P, S // 16], U16, name="places")
         nc.sync.dma_start(picks[:], offs)
 
+        tab_sc = held("tab_sc", K_PASSES * T, U8)
+        wk_sc_raw = held("wk_sc_raw", K_PASSES * H, U8, tag="wk_sc_then_wgo")
+        wv_sc_raw = held("wv_sc_raw", N, U8)
+        for plane in (tab_sc, wk_sc_raw, wv_sc_raw):
+            nc.vector.memset(plane[:].bitcast(I32), 0)
+        pages = [held("page0", T2, F32), held("page1", T2, F32)]
+        for page in pages:
+            nc.vector.memset(page[:], 0.0)
+
+        def load_scale_rows(plane, scales):
+            for q in range(QUADS):
+                nc.sync.dma_start(
+                    plane[32 * q : 32 * q + 4, :].bitcast(I32).rearrange("r (a w) -> r a w", a=K_PASSES),
+                    scales[:, 4 * q : 4 * q + 4, :].bitcast(I32).rearrange("a r w -> r a w"),
+                )
+
+        tab = [held(f"tab{a}", T, I32, tag=f"pass_raw{a}") for a in range(K_PASSES)]
         wk_raw = held("wk_raw", K_PASSES * 2 * H, U8, tag="weight_raw")
+        nc.sync.dma_start(tab[0][:], tab_words[0].rearrange("p t i -> p (t i)").bitcast(I32))
+        load_scale_rows(tab_sc, tab_scales)
         nc.sync.dma_start(
             wk_raw[:].bitcast(I32).rearrange("p (a w) -> p a w", a=K_PASSES),
             wk_words.bitcast(I32).rearrange("a p w -> p a w"),
         )
-        tab = [held(f"tab{a}", T, I32, tag=f"pass_raw{a}") for a in range(K_PASSES)]
-        for a in range(K_PASSES):
-            nc.sync.dma_start(tab[a][:], tab_words[a].rearrange("p t i -> p (t i)").bitcast(I32))
-        nc.sync.dma_start(places[:], offs2)
-
-        tab_sc = held("tab_sc", K_PASSES * T, U8)
-        wk_sc_raw = held("wk_sc_raw", K_PASSES * H, U8, tag="wk_sc_then_wgo")
-        wv_sc_raw = held("wv_sc_raw", N, U8)
-        for plane in (wk_sc_raw, tab_sc, wv_sc_raw):
-            nc.vector.memset(plane[:].bitcast(I32), 0)
-        for q in range(QUADS):
-            nc.scalar.dma_start(
-                tab_sc[32 * q : 32 * q + 4, :].bitcast(I32).rearrange("r (a w) -> r a w", a=K_PASSES),
-                tab_scales[:, 4 * q : 4 * q + 4, :].bitcast(I32).rearrange("a r w -> r a w"),
-            )
-        for q in range(QUADS):
-            nc.gpsimd.dma_start(
-                wk_sc_raw[32 * q : 32 * q + 4, :].bitcast(I32).rearrange("r (a w) -> r a w", a=K_PASSES),
-                wk_scales[:, 4 * q : 4 * q + 4, :].bitcast(I32).rearrange("a r w -> r a w"),
-            )
-        for q in range(QUADS):
-            nc.gpsimd.dma_start(
-                wv_sc_raw[32 * q : 32 * q + 4 * H_PASSES, :].bitcast(I32),
-                wv_scales[:, 4 * q : 4 * q + 4, :].bitcast(I32),
-            )
-
-        pages = [held("page0", T2, F32), held("page1", T2, F32)]
-        for page in pages:
-            nc.vector.memset(page[:, : T2 // 2 - 1], 0.0)
-            nc.vector.memset(page[:, T2 // 2 - 1 :], 0.0)
+        load_scale_rows(wk_sc_raw, wk_scales)
+        nc.sync.dma_start(tab[1][:], tab_words[1].rearrange("p t i -> p (t i)").bitcast(I32))
 
         wk_codes = [held(f"wk_codes{b}", K_PASSES * 2 * PASS, U8) for b in range(H_PASSES)]
         wk_sc = [held(f"wk_sc{b}", K_PASSES * PASS, U8) for b in range(H_PASSES)]
@@ -100,21 +92,31 @@ def tile_list_rwkv_channel_mix_kernel(
                 wk_sc_raw[:].rearrange("p (a b q t) -> p b a q t", a=K_PASSES, b=H_PASSES, t=PACK)[:, b],
             )
 
-        def gather_codes(a):
-            nc.vector.tensor_copy(v_codes[a][:], tab[a][:].bitcast(U32).indirect(picks[:]))
+        def tokens(h):
+            return slice(h * HALF, (h + 1) * HALF)
 
-        def gather_scales(a):
-            nc.vector.tensor_copy(v_sc[a][:], tab_sc[:, a * T : (a + 1) * T].indirect(picks[:]))
+        def entries(h):
+            return slice(h * HALF // 16, (h + 1) * HALF // 16)
+
+        def gather_codes(a, h):
+            nc.vector.tensor_copy(v_codes[a][:, tokens(h)], tab[a][:].bitcast(U32).indirect(picks[:, entries(h)]))
+
+        def gather_scales(a, h):
+            nc.vector.tensor_copy(v_sc[a][:, tokens(h)], tab_sc[:, a * T : (a + 1) * T].indirect(picks[:, entries(h)]))
 
         for b in range(H_PASSES):
             deal_wk_codes(b)
-        gather_scales(0)
-        gather_codes(0)
+        gather_codes(0, 0)
+        gather_scales(0, 0)
+        gather_scales(1, 0)
+        gather_codes(0, 1)
         deal_wk_scales(0)
-        gather_scales(1)
-        gather_codes(1)
-        for b in range(1, H_PASSES):
-            deal_wk_scales(b)
+        gather_scales(0, 1)
+        gather_codes(1, 0)
+        deal_wk_scales(1)
+        gather_codes(1, 1)
+        deal_wk_scales(2)
+        gather_scales(1, 1)
 
         wr_codes = {}
         wr_sc = {}
@@ -151,16 +153,27 @@ def tile_list_rwkv_channel_mix_kernel(
                 .rearrange("b p w -> p b w"),
             )
 
-        def deal_wv_codes(g):
+        def deal_wv_codes(g, on_scalar):
             wv_codes[g] = held(f"wv_codes{g}", H_PASSES * PASS, I32)
-            nc.vector.tensor_copy(
-                wv_codes[g][:].rearrange("p (b t q) -> p b q t", b=H_PASSES, t=PACK),
-                wv_raw[g][:].rearrange("p (b q t) -> p b q t", b=H_PASSES, t=PACK),
-            )
+            dst = wv_codes[g][:].rearrange("p (b t q) -> p b q t", b=H_PASSES, t=PACK)
+            src = wv_raw[g][:].rearrange("p (b q t) -> p b q t", b=H_PASSES, t=PACK)
+            if on_scalar:
+                nc.scalar.copy(
+                    wv_codes[g][:].bitcast(U32).rearrange("p (b t q) -> p b q t", b=H_PASSES, t=PACK),
+                    wv_raw[g][:].bitcast(U32).rearrange("p (b q t) -> p b q t", b=H_PASSES, t=PACK),
+                )
+            else:
+                nc.vector.tensor_copy(dst, src)
 
         load_wr(0, 0)
         load_wv(0)
         load_wr(1, 0)
+        for q in range(QUADS):
+            nc.sync.dma_start(
+                wv_sc_raw[32 * q : 32 * q + 4 * H_PASSES, :].bitcast(I32),
+                wv_scales[:, 4 * q : 4 * q + 4, :].bitcast(I32),
+            )
+        nc.sync.dma_start(places[:], offs2)
         gains = held("gains", PACK * S, F32, tag="wk_sc_then_wgo")
         for q in range(QUADS):
             nc.sync.dma_start(gains[32 * q : 32 * q + 32, :], wgo.rearrange("(p t) j -> p (t j)", t=PACK))
@@ -168,129 +181,122 @@ def tile_list_rwkv_channel_mix_kernel(
         h_codes = [held(f"h_codes{b}", S, U32) for b in range(H_PASSES)]
         h_sc = [held(f"h_sc{b}", S, U8) for b in range(H_PASSES)]
 
-        def key_group(b):
-            relu = held(f"relu{b}", PACK * S, F32, tag="relu", bufs=2)
-            for t in range(PACK):
-                acc = bank(f"key{b}{t}")
-                for a in range(K_PASSES):
-                    col = a * PASS + t * P
-                    nc.tensor.matmul_mx(
-                        out=acc[:],
-                        lhsT=wk_codes[b][:, 2 * col : 2 * (col + P)].bitcast(FP4X4),
-                        lhsT_scale=wk_sc[b][:, col : col + P],
-                        rhs=v_codes[a][:].bitcast(FP8X4),
-                        rhs_scale=v_sc[a][:],
-                        start=(a == 0),
-                        stop=(a == K_PASSES - 1),
-                    )
-                dst = relu[:, t * S : (t + 1) * S]
-                if PACK * b + t < RELU_ON_SCALAR:
+        def key_group(b, h, pairs_on_scalar):
+            relu = held(f"relu{b}{h}", PACK * HALF, F32, tag="relu", bufs=3)
+            for u in range(PAIRS):
+                acc = bank(f"key{b}{h}{u}", "key", 4)
+                for e in range(2):
+                    for a in range(K_PASSES):
+                        col = a * PASS + (2 * u + e) * P
+                        nc.tensor.matmul_mx(
+                            out=acc[:, e * HALF : (e + 1) * HALF],
+                            lhsT=wk_codes[b][:, 2 * col : 2 * (col + P)].bitcast(FP4X4),
+                            lhsT_scale=wk_sc[b][:, col : col + P],
+                            rhs=v_codes[a][:, tokens(h)].bitcast(FP8X4),
+                            rhs_scale=v_sc[a][:, tokens(h)],
+                            start=(a == 0),
+                            stop=(a == K_PASSES - 1),
+                        )
+                dst = relu[:, u * S : (u + 1) * S]
+                if u < pairs_on_scalar:
                     nc.scalar.activation(dst, acc[:], ACT.Relu)
                 else:
                     nc.vector.tensor_scalar_max(dst, acc[:], 0.0)
             return relu
 
-        def square_group(b, relu):
-            h_bf = held(f"h_bf{b}", PACK * S, BF16)
-            src = relu[:].rearrange("p (t c i) -> p c t i", t=PACK, i=4)
-            dst = h_bf[:].rearrange("p (c i t) -> p c t i", t=PACK, i=4)
-            if b < H_PASSES - 1:
-                nc.scalar.activation(dst, src, ACT.Square)
+        def square_group(b, h, relu):
+            if (b, h) == (H_PASSES - 1, 0):
+                h_bf = held(f"h_bf{b}{h}", PACK * HALF, BF16, tag="h_bf_then_page")
             else:
-                half = S // 4 // 2
-                nc.scalar.activation(dst[:, :half], src[:, :half], ACT.Square)
-                nc.vector.tensor_tensor(dst[:, half:], src[:, half:], src[:, half:], ALU.mult)
-            return h_bf
+                h_bf = held(f"h_bf{b}{h}", PACK * HALF, BF16, tag="h_bf", bufs=3)
+            nc.scalar.activation(
+                h_bf[:].rearrange("p (c i t) -> p c t i", t=PACK, i=4),
+                relu[:].rearrange("p (t c i) -> p c t i", t=PACK, i=4),
+                ACT.Square,
+            )
+            nc.vector.quantize_mx(
+                out=h_codes[b][:, tokens(h)].bitcast(FP8X4), scales=h_sc[b][:, tokens(h)], in_=h_bf[:]
+            )
 
-        def quantize_h(b, h_bf):
-            nc.vector.quantize_mx(out=h_codes[b][:].bitcast(FP8X4), scales=h_sc[b][:], in_=h_bf[:])
-
-        gates = {}
-
-        def gate(i):
-            g, t = divmod(i, PACK)
-            acc = bank(f"rec{i}")
+        def rec_passes(acc, g, t, cols):
             for a in range(K_PASSES):
                 nc.tensor.matmul_mx(
-                    out=acc[:],
+                    out=acc,
                     lhsT=wr_codes[a, g][:, t * P : (t + 1) * P].bitcast(FP8X4),
                     lhsT_scale=wr_sc[a, g][:, t * P : (t + 1) * P],
-                    rhs=v_codes[a][:].bitcast(FP8X4),
-                    rhs_scale=v_sc[a][:],
+                    rhs=v_codes[a][:, cols].bitcast(FP8X4),
+                    rhs_scale=v_sc[a][:, cols],
                     start=(a == 0),
                     stop=(a == K_PASSES - 1),
                 )
-            if i == 0:
-                gates[i] = held("gate0", S, F32, tag="gate0_then_page")
-            else:
-                gates[i] = held(f"gate{i}", S, F32, tag="gate", bufs=3)
-            nc.scalar.activation(gates[i][:], acc[:], ACT.Sigmoid)
 
-        relu0 = key_group(0)
-        quantize_wr(0, 0, False)
-        h_bf0 = square_group(0, relu0)
-        deal_wv_codes(0)
-        wv_sc = held("wv_sc", N, U8)
-        nc.vector.tensor_copy(
-            wv_sc[:].rearrange("p (g t q) -> p g q t", g=N_GROUPS, t=PACK),
-            wv_sc_raw[:].rearrange("p (g q t) -> p g q t", g=N_GROUPS, t=PACK),
-        )
-        load_wv(1)
-        load_wr(0, 1)
-        relu1 = key_group(1)
-        quantize_h(0, h_bf0)
-        quantize_wr(1, 0, False)
-        load_wr(1, 1)
-        h_bf1 = square_group(1, relu1)
-        relu2 = key_group(2)
-        gate(0)
-        quantize_h(1, h_bf1)
-        h_bf2 = square_group(2, relu2)
-        quantize_h(2, h_bf2)
-        pages.append(held("page2", T2, F32, tag="h_bf2"))
-        nc.gpsimd.memset(pages[2][:], 0.0)
-
-        gated = {}
-
-        def value(i):
-            g, t = divmod(i, PACK)
-            acc = bank(f"val{i}")
+        def val_passes(acc, g, t, cols):
             for b in range(H_PASSES):
                 col = b * PASS + t * P
                 nc.tensor.matmul_mx(
-                    out=acc[:],
+                    out=acc,
                     lhsT=wv_codes[g][:, col : col + P].bitcast(FP8X4),
                     lhsT_scale=wv_sc[4 * b :, g * PASS + t * P : g * PASS + (t + 1) * P],
-                    rhs=h_codes[b][:].bitcast(FP8X4),
-                    rhs_scale=h_sc[b][:],
+                    rhs=h_codes[b][:, cols].bitcast(FP8X4),
+                    rhs_scale=h_sc[b][:, cols],
                     start=(b == 0),
                     stop=(b == H_PASSES - 1),
                 )
-            gated[i] = held(f"gated{i}", S, F32, tag="gated", bufs=3)
-            nc.vector.tensor_tensor(gated[i][:], acc[:], gates[i][:], ALU.mult)
+
+        steps = [[(0, 2 * u + e, h) for e in range(2)] for h in range(HALVES) for u in range(PAIRS)]
+        steps = steps + [[(1, t, None)] for t in range(PACK)]
+        gates = {}
+        gated = {}
+
+        def piece_cols(h):
+            return slice(0, S) if h is None else tokens(h)
+
+        def fill(acc, passes, k):
+            width = S // len(steps[k])
+            for e, (g, t, h) in enumerate(steps[k]):
+                passes(acc[:, e * width : (e + 1) * width], g, t, piece_cols(h))
+
+        def gate(k):
+            acc = bank(f"rec{k}", "rec", 2)
+            fill(acc, rec_passes, k)
+            gates[k] = held(f"gate{k}", S, F32, tag="gate0_then_page" if k == 0 else f"gate{k}")
+            nc.scalar.activation(gates[k][:], acc[:], ACT.Sigmoid)
+
+        def value(k):
+            acc = bank(f"val{k}", "val", 2)
+            fill(acc, val_passes, k)
+            if k == len(steps) - 1:
+                gated[k] = held(f"gated{k}", S, F32, tag=f"woven{CHUNKS - 1}")
+            else:
+                gated[k] = held(f"gated{k}", S, F32, tag="gated", bufs=3)
+            nc.vector.tensor_tensor(gated[k][:], acc[:], gates[k][:], ALU.mult)
 
         out_rows = out_0.rearrange("(g p t) m -> g t p m", t=PACK, p=P)
 
-        def scatter(i):
-            g, t = divmod(i, PACK)
-            page = pages[i % PAGES]
-            nc.vector.tensor_tensor(
-                page[:].indirect(places[:]), gated[i][:], gains[:, t * S : (t + 1) * S], ALU.mult
-            )
-            nc.sync.dma_start(out_rows[g, t], page[:])
+        def scatter(k):
+            width = S // len(steps[k])
+            for e, (g, t, h) in enumerate(steps[k]):
+                offsets = places[:] if h is None else places[:, entries(h)]
+                first = t * S + piece_cols(h).start
+                nc.vector.tensor_tensor(
+                    pages[t][:].indirect(offsets),
+                    gated[k][:, e * width : (e + 1) * width],
+                    gains[:, first : first + width],
+                    ALU.mult,
+                )
+                if h != 0:
+                    nc.sync.dma_start(out_rows[g, t], pages[t][:])
 
-        pairs = {}
-
-        def on_vector(i, c):
-            return i >= N_GROUPS * PACK - 2 and c < TAIL_CHUNKS_ON_VECTOR
+        last = N_GROUPS * PACK - 1
+        rounded_rows = {}
 
         def round_page(i, c):
             g, t = divmod(i, PACK)
             if t == 0:
-                pairs[g, c] = held(f"pairs{g}{c}", PACK * CHUNK, BF16, tag=f"pairs{c}")
-            dst = pairs[g, c][:].rearrange("p (u m e) -> p u m e", u=2, e=2)[:, t // 2, :, t % 2]
+                rounded_rows[g, c] = held(f"rows{g}{c}", PACK * CHUNK, BF16, tag=f"rows{g}{c}")
+            dst = rounded_rows[g, c][:, t * CHUNK : (t + 1) * CHUNK]
             src = pages[i % PAGES][:, c * CHUNK : (c + 1) * CHUNK]
-            if on_vector(i, c):
+            if i == last:
                 nc.vector.tensor_copy(dst, src)
             else:
                 nc.scalar.copy(dst, src)
@@ -298,17 +304,13 @@ def tile_list_rwkv_channel_mix_kernel(
         y_sc = {}
 
         def planes(g, c):
-            woven = held(f"woven{g}{c}", PACK * CHUNK, BF16, tag="woven", bufs=3)
-            if on_vector(PACK * g + PACK - 1, c):
-                nc.vector.tensor_copy(
-                    woven[:].bitcast(I32).rearrange("p (m u) -> p m u", u=2),
-                    pairs[g, c][:].bitcast(I32).rearrange("p (u m) -> p m u", u=2),
-                )
+            woven = held(f"woven{g}{c}", PACK * CHUNK, BF16, tag=f"woven{c}")
+            dst = woven[:].rearrange("p (c i t) -> p c t i", t=PACK, i=4)
+            src = rounded_rows[g, c][:].rearrange("p (t c i) -> p c t i", t=PACK, i=4)
+            if g == N_GROUPS - 1 and c % 2 == 0:
+                nc.vector.tensor_copy(dst, src)
             else:
-                nc.scalar.copy(
-                    woven[:].bitcast(U32).rearrange("p (m u) -> p m u", u=2),
-                    pairs[g, c][:].bitcast(U32).rearrange("p (u m) -> p m u", u=2),
-                )
+                nc.scalar.copy(dst, src)
             if c == 0:
                 y_sc[g] = held(f"y_sc{g}", CHUNK, U8)
             codes = held(f"y_codes{g}{c}", CHUNK, I32, tag="y_codes", bufs=4)
@@ -324,26 +326,71 @@ def tile_list_rwkv_channel_mix_kernel(
                     y_sc[g][32 * q : 32 * q + 4 * CHUNKS, :].bitcast(I32),
                 )
 
-        last = N_GROUPS * PACK - 1
-        value(0)
-        gate(1)
-        pages.append(held("page3", T2, F32, tag="gate0_then_page"))
-        nc.gpsimd.memset(pages[3][:], 0.0)
-        for i in range(last + 1):
-            if i < last:
-                value(i + 1)
-            if i + 2 <= last:
-                gate(i + 2)
-            scatter(i)
-            if i == 0:
-                quantize_wr(0, 1, True)
-                deal_wv_codes(1)
-            if i == 1:
-                quantize_wr(1, 1, False)
+        def round_whole_page(i):
             for c in range(CHUNKS):
                 round_page(i, c)
-                if i % PACK == PACK - 1:
-                    planes(i // PACK, c)
-            if i == PACK - 1:
-                store_scales(0, nc.sync)
+
+        wv_sc = held("wv_sc", N, U8)
+
+        relu = key_group(0, 0, 2)
+        quantize_wr(0, 0, False)
+        square_group(0, 0, relu)
+        deal_wv_codes(0, False)
+        nc.vector.tensor_copy(
+            wv_sc[:].rearrange("p (g t q) -> p g q t", g=N_GROUPS, t=PACK),
+            wv_sc_raw[:].rearrange("p (g q t) -> p g q t", g=N_GROUPS, t=PACK),
+        )
+        load_wv(1)
+        load_wr(0, 1)
+        relu = key_group(1, 0, 2)
+        quantize_wr(1, 0, False)
+        load_wr(1, 1)
+        square_group(1, 0, relu)
+        relu = key_group(2, 0, 2)
+        gate(0)
+        square_group(2, 0, relu)
+        pages.append(held("page2", T2, F32, tag="h_bf_then_page"))
+        nc.gpsimd.memset(pages[2][:], 0.0)
+        value(0)
+        pages.append(held("page3", T2, F32, tag="gate0_then_page"))
+        nc.gpsimd.memset(pages[3][:], 0.0)
+        gate(1)
+        scatter(0)
+        value(1)
+        for b in range(H_PASSES):
+            square_group(b, 1, key_group(b, 1, 2))
+        scatter(1)
+        gate(2)
+        gate(3)
+        value(2)
+        value(3)
+        scatter(2)
+        quantize_wr(0, 1, True)
+        deal_wv_codes(1, True)
+        quantize_wr(1, 1, True)
+        scatter(3)
+        gate(4)
+        round_whole_page(0)
+        value(4)
+        gate(5)
+        round_whole_page(1)
+        scatter(4)
+        value(5)
+        gate(6)
+        round_whole_page(2)
+        scatter(5)
+        value(6)
+        gate(7)
+        round_whole_page(3)
+        scatter(6)
+        for c in range(CHUNKS):
+            planes(0, c)
+        store_scales(0, nc.sync)
+        value(7)
+        for i in range(PACK, last):
+            round_whole_page(i)
+        scatter(7)
+        round_whole_page(last)
+        for c in range(CHUNKS):
+            planes(1, c)
         store_scales(1, nc.scalar)

@@ -57,9 +57,9 @@ def tile_list_rwkv_channel_mix_kernel(
         for page in pages:
             nc.vector.memset(page[:], 0.0)
 
-        def load_scale_rows(plane, scales):
+        def load_scale_rows(queue, plane, scales):
             for q in range(QUADS):
-                nc.sync.dma_start(
+                queue.dma_start(
                     plane[32 * q : 32 * q + 4, :].bitcast(I32).rearrange("r (a w) -> r a w", a=K_PASSES),
                     scales[:, 4 * q : 4 * q + 4, :].bitcast(I32).rearrange("a r w -> r a w"),
                 )
@@ -67,13 +67,13 @@ def tile_list_rwkv_channel_mix_kernel(
         tab = [held(f"tab{a}", T, I32, tag=f"pass_raw{a}") for a in range(K_PASSES)]
         wk_raw = held("wk_raw", K_PASSES * 2 * H, U8, tag="weight_raw")
         nc.sync.dma_start(tab[0][:], tab_words[0].rearrange("p t i -> p (t i)").bitcast(I32))
-        load_scale_rows(tab_sc, tab_scales)
+        load_scale_rows(nc.sync, tab_sc, tab_scales)
+        nc.sync.dma_start(tab[1][:], tab_words[1].rearrange("p t i -> p (t i)").bitcast(I32))
         nc.sync.dma_start(
             wk_raw[:].bitcast(I32).rearrange("p (a w) -> p a w", a=K_PASSES),
             wk_words.bitcast(I32).rearrange("a p w -> p a w"),
         )
-        load_scale_rows(wk_sc_raw, wk_scales)
-        nc.sync.dma_start(tab[1][:], tab_words[1].rearrange("p t i -> p (t i)").bitcast(I32))
+        load_scale_rows(nc.sync, wk_sc_raw, wk_scales)
 
         wk_codes = [held(f"wk_codes{b}", K_PASSES * 2 * PASS, U8) for b in range(H_PASSES)]
         wk_sc = [held(f"wk_sc{b}", K_PASSES * PASS, U8) for b in range(H_PASSES)]
@@ -101,22 +101,19 @@ def tile_list_rwkv_channel_mix_kernel(
         def gather_codes(a, h):
             nc.vector.tensor_copy(v_codes[a][:, tokens(h)], tab[a][:].bitcast(U32).indirect(picks[:, entries(h)]))
 
-        def gather_scales(a, h):
-            nc.vector.tensor_copy(v_sc[a][:, tokens(h)], tab_sc[:, a * T : (a + 1) * T].indirect(picks[:, entries(h)]))
+        def gather_scales(a):
+            nc.vector.tensor_copy(v_sc[a][:], tab_sc[:, a * T : (a + 1) * T].indirect(picks[:]))
 
         for b in range(H_PASSES):
             deal_wk_codes(b)
-        gather_codes(0, 0)
-        gather_scales(0, 0)
-        gather_scales(1, 0)
-        gather_codes(0, 1)
-        deal_wk_scales(0)
-        gather_scales(0, 1)
+        nc.vector.tensor_copy(v_codes[0][:], tab[0][:].bitcast(U32).indirect(picks[:]))
+        gather_scales(0)
+        gather_scales(1)
         gather_codes(1, 0)
-        deal_wk_scales(1)
+        deal_wk_scales(0)
         gather_codes(1, 1)
+        deal_wk_scales(1)
         deal_wk_scales(2)
-        gather_scales(1, 1)
 
         wr_codes = {}
         wr_sc = {}
@@ -132,7 +129,8 @@ def tile_list_rwkv_channel_mix_kernel(
             )
 
         def quantize_wr(a, g, on_scalar):
-            rounded = held(f"wr_bf{a}{g}", PACK * PASS, BF16, tag="wr_bf", bufs=2)
+            tag = f"wr_bf{a}" if g == 0 else ("relu_half1", "h_bf_last")[a]
+            rounded = held(f"wr_bf{a}{g}", PACK * PASS, BF16, tag=tag)
             dst = rounded[:].rearrange("p (t m j) -> p m j t", t=PACK, j=PACK)
             src = wr_raw[a, g][:].rearrange("p (j m t) -> p m j t", j=PACK, t=PACK)
             if on_scalar:
@@ -144,7 +142,7 @@ def tile_list_rwkv_channel_mix_kernel(
             nc.vector.quantize_mx(out=wr_codes[a, g][:].bitcast(FP8X4), scales=wr_sc[a, g][:], in_=rounded[:])
 
         def load_wv(g):
-            wv_raw[g] = held(f"wv_raw{g}", H_PASSES * PASS, I32, tag="weight_raw")
+            wv_raw[g] = held(f"wv_raw{g}", H_PASSES * PASS, I32, tag="weight_raw" if g else "wv_raw0")
             nc.sync.dma_start(
                 wv_raw[g][:].rearrange("p (b w) -> p b w", b=H_PASSES),
                 wv_words[:, :, g * PASS : (g + 1) * PASS, :]
@@ -154,7 +152,7 @@ def tile_list_rwkv_channel_mix_kernel(
             )
 
         def deal_wv_codes(g, on_scalar):
-            wv_codes[g] = held(f"wv_codes{g}", H_PASSES * PASS, I32)
+            wv_codes[g] = held(f"wv_codes{g}", H_PASSES * PASS, I32, tag="h_bf_then_wv" if g else "wv_codes0")
             dst = wv_codes[g][:].rearrange("p (b t q) -> p b q t", b=H_PASSES, t=PACK)
             src = wv_raw[g][:].rearrange("p (b q t) -> p b q t", b=H_PASSES, t=PACK)
             if on_scalar:
@@ -166,25 +164,25 @@ def tile_list_rwkv_channel_mix_kernel(
                 nc.vector.tensor_copy(dst, src)
 
         load_wr(0, 0)
-        load_wv(0)
-        load_wr(1, 0)
         for q in range(QUADS):
             nc.sync.dma_start(
                 wv_sc_raw[32 * q : 32 * q + 4 * H_PASSES, :].bitcast(I32),
                 wv_scales[:, 4 * q : 4 * q + 4, :].bitcast(I32),
             )
+        load_wv(0)
+        load_wr(1, 0)
         nc.sync.dma_start(places[:], offs2)
         gains = held("gains", PACK * S, F32, tag="wk_sc_then_wgo")
         for q in range(QUADS):
-            nc.sync.dma_start(gains[32 * q : 32 * q + 32, :], wgo.rearrange("(p t) j -> p (t j)", t=PACK))
+            nc.gpsimd.dma_start(gains[32 * q : 32 * q + 32, :], wgo.rearrange("(p t) j -> p (t j)", t=PACK))
 
         h_codes = [held(f"h_codes{b}", S, U32) for b in range(H_PASSES)]
         h_sc = [held(f"h_sc{b}", S, U8) for b in range(H_PASSES)]
 
         def key_group(b, h, pairs_on_scalar):
-            relu = held(f"relu{b}{h}", PACK * HALF, F32, tag="relu", bufs=3)
+            relu = held(f"relu{b}{h}", PACK * HALF, F32, tag=f"relu_half{h}", bufs=2 - h)
             for u in range(PAIRS):
-                acc = bank(f"key{b}{h}{u}", "key", 4)
+                acc = bank(f"key{b}{h}{u}", "short", 2) if (b, h) == (0, 1) else bank(f"key{b}{h}{u}", "key", 4)
                 for e in range(2):
                     for a in range(K_PASSES):
                         col = a * PASS + (2 * u + e) * P
@@ -205,8 +203,10 @@ def tile_list_rwkv_channel_mix_kernel(
             return relu
 
         def square_group(b, h, relu):
-            if (b, h) == (H_PASSES - 1, 0):
-                h_bf = held(f"h_bf{b}{h}", PACK * HALF, BF16, tag="h_bf_then_page")
+            if (b, h) == (H_PASSES - 1, 1):
+                h_bf = held(f"h_bf{b}{h}", PACK * HALF, BF16, tag="h_bf_last")
+            elif (b, h) == (H_PASSES - 2, 1):
+                h_bf = held(f"h_bf{b}{h}", PACK * HALF, BF16, tag="h_bf_then_wv")
             else:
                 h_bf = held(f"h_bf{b}{h}", PACK * HALF, BF16, tag="h_bf", bufs=3)
             nc.scalar.activation(
@@ -218,30 +218,28 @@ def tile_list_rwkv_channel_mix_kernel(
                 out=h_codes[b][:, tokens(h)].bitcast(FP8X4), scales=h_sc[b][:, tokens(h)], in_=h_bf[:]
             )
 
-        def rec_passes(acc, g, t, cols):
-            for a in range(K_PASSES):
-                nc.tensor.matmul_mx(
-                    out=acc,
-                    lhsT=wr_codes[a, g][:, t * P : (t + 1) * P].bitcast(FP8X4),
-                    lhsT_scale=wr_sc[a, g][:, t * P : (t + 1) * P],
-                    rhs=v_codes[a][:, cols].bitcast(FP8X4),
-                    rhs_scale=v_sc[a][:, cols],
-                    start=(a == 0),
-                    stop=(a == K_PASSES - 1),
-                )
+        def rec_pass(acc, a, g, t, cols, start, stop):
+            nc.tensor.matmul_mx(
+                out=acc,
+                lhsT=wr_codes[a, g][:, t * P : (t + 1) * P].bitcast(FP8X4),
+                lhsT_scale=wr_sc[a, g][:, t * P : (t + 1) * P],
+                rhs=v_codes[a][:, cols].bitcast(FP8X4),
+                rhs_scale=v_sc[a][:, cols],
+                start=start,
+                stop=stop,
+            )
 
-        def val_passes(acc, g, t, cols):
-            for b in range(H_PASSES):
-                col = b * PASS + t * P
-                nc.tensor.matmul_mx(
-                    out=acc,
-                    lhsT=wv_codes[g][:, col : col + P].bitcast(FP8X4),
-                    lhsT_scale=wv_sc[4 * b :, g * PASS + t * P : g * PASS + (t + 1) * P],
-                    rhs=h_codes[b][:, cols].bitcast(FP8X4),
-                    rhs_scale=h_sc[b][:, cols],
-                    start=(b == 0),
-                    stop=(b == H_PASSES - 1),
-                )
+        def val_pass(acc, b, g, t, cols, start, stop):
+            col = b * PASS + t * P
+            nc.tensor.matmul_mx(
+                out=acc,
+                lhsT=wv_codes[g][:, col : col + P].bitcast(FP8X4),
+                lhsT_scale=wv_sc[4 * b :, g * PASS + t * P : g * PASS + (t + 1) * P],
+                rhs=h_codes[b][:, cols].bitcast(FP8X4),
+                rhs_scale=h_sc[b][:, cols],
+                start=start,
+                stop=stop,
+            )
 
         steps = [[(0, 2 * u + e, h) for e in range(2)] for h in range(HALVES) for u in range(PAIRS)]
         steps = steps + [[(1, t, None)] for t in range(PACK)]
@@ -251,22 +249,27 @@ def tile_list_rwkv_channel_mix_kernel(
         def piece_cols(h):
             return slice(0, S) if h is None else tokens(h)
 
-        def fill(acc, passes, k):
-            width = S // len(steps[k])
-            for e, (g, t, h) in enumerate(steps[k]):
-                passes(acc[:, e * width : (e + 1) * width], g, t, piece_cols(h))
+        def fill(acc, one_pass, passes, k):
+            pieces = len(steps[k])
+            width = S // pieces
+            for n in range(passes):
+                for e, (g, t, h) in enumerate(steps[k]):
+                    first, final = (n, e) == (0, 0), (n, e) == (passes - 1, pieces - 1)
+                    one_pass(acc[:, e * width : (e + 1) * width], n, g, t, piece_cols(h), first, final)
 
         def gate(k):
-            acc = bank(f"rec{k}", "rec", 2)
-            fill(acc, rec_passes, k)
-            gates[k] = held(f"gate{k}", S, F32, tag="gate0_then_page" if k == 0 else f"gate{k}")
+            acc = bank(f"rec{k}", "short", 2)
+            fill(acc, rec_pass, K_PASSES, k)
+            gates[k] = held(f"gate{k}", S, F32, tag=f"gate{k}")
             nc.scalar.activation(gates[k][:], acc[:], ACT.Sigmoid)
 
         def value(k):
             acc = bank(f"val{k}", "val", 2)
-            fill(acc, val_passes, k)
+            fill(acc, val_pass, H_PASSES, k)
             if k == len(steps) - 1:
                 gated[k] = held(f"gated{k}", S, F32, tag=f"woven{CHUNKS - 1}")
+            elif k == 3:
+                gated[k] = held(f"gated{k}", S, F32, tag="h_bf_last")
             else:
                 gated[k] = held(f"gated{k}", S, F32, tag="gated", bufs=3)
             nc.vector.tensor_tensor(gated[k][:], acc[:], gates[k][:], ALU.mult)
@@ -296,7 +299,7 @@ def tile_list_rwkv_channel_mix_kernel(
                 rounded_rows[g, c] = held(f"rows{g}{c}", PACK * CHUNK, BF16, tag=f"rows{g}{c}")
             dst = rounded_rows[g, c][:, t * CHUNK : (t + 1) * CHUNK]
             src = pages[i % PAGES][:, c * CHUNK : (c + 1) * CHUNK]
-            if i == last:
+            if i == last and c % 2 == 0:
                 nc.vector.tensor_copy(dst, src)
             else:
                 nc.scalar.copy(dst, src)
@@ -307,14 +310,14 @@ def tile_list_rwkv_channel_mix_kernel(
             woven = held(f"woven{g}{c}", PACK * CHUNK, BF16, tag=f"woven{c}")
             dst = woven[:].rearrange("p (c i t) -> p c t i", t=PACK, i=4)
             src = rounded_rows[g, c][:].rearrange("p (t c i) -> p c t i", t=PACK, i=4)
-            if g == N_GROUPS - 1 and c % 2 == 0:
+            if (g == N_GROUPS - 1 and c % 2 == 0) or (g, c) == (0, 0):
                 nc.vector.tensor_copy(dst, src)
             else:
                 nc.scalar.copy(dst, src)
             if c == 0:
-                y_sc[g] = held(f"y_sc{g}", CHUNK, U8)
+                y_sc[g] = held(f"y_sc{g}", T2, U8)
             codes = held(f"y_codes{g}{c}", CHUNK, I32, tag="y_codes", bufs=4)
-            nc.vector.quantize_mx(out=codes[:].bitcast(FP8X4), scales=y_sc[g][4 * c :, :], in_=woven[:])
+            nc.vector.quantize_mx(out=codes[:].bitcast(FP8X4), scales=y_sc[g][:, c * CHUNK : (c + 1) * CHUNK], in_=woven[:])
             nc.sync.dma_start(
                 out_1[g].rearrange("p m t -> p (m t)").bitcast(I32)[:, c * CHUNK : (c + 1) * CHUNK], codes[:]
             )
@@ -322,8 +325,8 @@ def tile_list_rwkv_channel_mix_kernel(
         def store_scales(g, queue):
             for q in range(QUADS):
                 queue.dma_start(
-                    out_2[g, 4 * q : 4 * q + 4, :].bitcast(I32).rearrange("r (c w) -> c r w", c=CHUNKS),
-                    y_sc[g][32 * q : 32 * q + 4 * CHUNKS, :].bitcast(I32),
+                    out_2[g, 4 * q : 4 * q + 4, :].bitcast(I32),
+                    y_sc[g][32 * q : 32 * q + 4, :].bitcast(I32),
                 )
 
         def round_whole_page(i):
@@ -340,46 +343,45 @@ def tile_list_rwkv_channel_mix_kernel(
             wv_sc[:].rearrange("p (g t q) -> p g q t", g=N_GROUPS, t=PACK),
             wv_sc_raw[:].rearrange("p (g q t) -> p g q t", g=N_GROUPS, t=PACK),
         )
-        load_wv(1)
         load_wr(0, 1)
         relu = key_group(1, 0, 2)
         quantize_wr(1, 0, False)
         load_wr(1, 1)
+        load_wv(1)
         square_group(1, 0, relu)
-        relu = key_group(2, 0, 2)
+        square_group(2, 0, key_group(2, 0, 2))
         gate(0)
-        square_group(2, 0, relu)
-        pages.append(held("page2", T2, F32, tag="h_bf_then_page"))
-        nc.gpsimd.memset(pages[2][:], 0.0)
         value(0)
-        pages.append(held("page3", T2, F32, tag="gate0_then_page"))
-        nc.gpsimd.memset(pages[3][:], 0.0)
+        pages.append(held("page2", T2, F32, tag="gate0"))
+        nc.gpsimd.memset(pages[2][:], 0.0)
         gate(1)
         scatter(0)
         value(1)
+        pages.append(held("page3", T2, F32, tag="gate1"))
+        nc.gpsimd.memset(pages[3][:], 0.0)
         for b in range(H_PASSES):
             square_group(b, 1, key_group(b, 1, 2))
         scatter(1)
         gate(2)
         gate(3)
         value(2)
-        value(3)
         scatter(2)
         quantize_wr(0, 1, True)
-        deal_wv_codes(1, True)
         quantize_wr(1, 1, True)
+        deal_wv_codes(1, False)
+        value(3)
         scatter(3)
-        gate(4)
         round_whole_page(0)
+        gate(4)
         value(4)
         gate(5)
+        value(5)
         round_whole_page(1)
         scatter(4)
-        value(5)
         gate(6)
+        value(6)
         round_whole_page(2)
         scatter(5)
-        value(6)
         gate(7)
         round_whole_page(3)
         scatter(6)
@@ -390,7 +392,7 @@ def tile_list_rwkv_channel_mix_kernel(
         for i in range(PACK, last):
             round_whole_page(i)
         scatter(7)
-        round_whole_page(last)
         for c in range(CHUNKS):
+            round_page(last, c)
             planes(1, c)
         store_scales(1, nc.scalar)

@@ -1,6 +1,7 @@
 from contextlib import ExitStack
 
 import concourse.mybir as mybir
+from concourse.masks import make_identity
 
 K, H, N, T, S, T2 = 1024, 1536, 1024, 2048, 512, 2048
 FLOPS = 2 * S * (K * H + K * N + H * N)
@@ -47,9 +48,13 @@ def tile_list_rwkv_channel_mix_kernel(
         picks = lists.tile([P, S // 16], U16, name="picks")
         places = lists.tile([P, S // 16], U16, name="places")
         nc.sync.dma_start(picks[:], offs)
+        wgo_rows = held("wgo_rows", S, F32)
+        nc.sync.dma_start(wgo_rows[:], wgo)
+        ident = held("ident", P, F32)
+        make_identity(nc, ident[:])
 
         tab_sc = held("tab_sc", K_PASSES * T, U8)
-        wk_sc_raw = held("wk_sc_raw", K_PASSES * H, U8, tag="wk_sc_then_wgo")
+        wk_sc_raw = held("wk_sc_raw", K_PASSES * H, U8)
         wv_sc_raw = held("wv_sc_raw", N, U8)
         for plane in (tab_sc, wk_sc_raw, wv_sc_raw):
             nc.vector.memset(plane[:].bitcast(I32), 0)
@@ -74,6 +79,26 @@ def tile_list_rwkv_channel_mix_kernel(
             wk_words.bitcast(I32).rearrange("a p w -> p a w"),
         )
         load_scale_rows(nc.sync, wk_sc_raw, wk_scales)
+
+        blocks = S // P
+        wgo_turned = bank("wgo_turned", "short", 2)
+        for n in range(blocks):
+            nc.tensor.transpose(wgo_turned[:, n * P : (n + 1) * P], wgo_rows[:, n * P : (n + 1) * P], ident[:])
+        gains = held("gains", PACK * S, F32)
+        dealt = [held(f"wgo_dealt{t}", S, F32, tag=f"rows0{t}") for t in range(PACK)]
+        for t in range(PACK):
+            nc.scalar.copy(
+                dealt[t][:].rearrange("j (n q r) -> j n q r", n=blocks, q=QUADS),
+                wgo_turned[:]
+                .rearrange("j (n r t) -> j t n r", n=blocks, t=PACK)[:, t]
+                .unsqueeze(2)
+                .broadcast_to([P, blocks, QUADS, P // QUADS]),
+            )
+        for t in range(PACK):
+            acc = bank(f"gains{t}", "key", 4)
+            for n in range(blocks):
+                nc.tensor.transpose(acc[:, n * P : (n + 1) * P], dealt[t][:, n * P : (n + 1) * P], ident[:])
+            nc.scalar.copy(gains[:, t * S : (t + 1) * S], acc[:])
 
         wk_codes = [held(f"wk_codes{b}", K_PASSES * 2 * PASS, U8) for b in range(H_PASSES)]
         wk_sc = [held(f"wk_sc{b}", K_PASSES * PASS, U8) for b in range(H_PASSES)]
@@ -172,9 +197,6 @@ def tile_list_rwkv_channel_mix_kernel(
         load_wv(0)
         load_wr(1, 0)
         nc.sync.dma_start(places[:], offs2)
-        gains = held("gains", PACK * S, F32, tag="wk_sc_then_wgo")
-        for q in range(QUADS):
-            nc.gpsimd.dma_start(gains[32 * q : 32 * q + 32, :], wgo.rearrange("(p t) j -> p (t j)", t=PACK))
 
         h_codes = [held(f"h_codes{b}", S, U32) for b in range(H_PASSES)]
         h_sc = [held(f"h_sc{b}", S, U8) for b in range(H_PASSES)]

from contextlib import ExitStack

import concourse.mybir as mybir
from concourse.masks import make_identity

K, H, N, T, S, T2 = 1024, 1536, 1024, 2048, 512, 2048
FLOPS = 2 * S * (K * H + K * N + H * N)

F32 = mybir.dt.float32
BF16 = mybir.dt.bfloat16
I32 = mybir.dt.int32
U32 = mybir.dt.uint32
U16 = mybir.dt.uint16
U8 = mybir.dt.uint8
FP8X4 = mybir.dt.float8_e4m3fn_x4
FP4X4 = mybir.dt.float4_e2m1fn_x4
ACT = mybir.ActivationFunctionType
ALU = mybir.AluOpType

P = 128
PACK = 4
PASS = P * PACK
QUADS = 4
K_PASSES, H_PASSES, N_GROUPS = K // PASS, H // PASS, N // PASS
CHUNK = 512
CHUNKS = T2 // CHUNK
PAGES = 4
HALVES = 2
HALF = S // HALVES
PAIRS = PACK // 2


def tile_list_rwkv_channel_mix_kernel(
    tc, tab_words, tab_scales, offs, wk_words, wk_scales, wr, wv_words, wv_scales, wgo, offs2, out_0, out_1, out_2
):
    nc = tc.nc
    with ExitStack() as ctx:
        lists = ctx.enter_context(tc.tile_pool(name="lists", bufs=1))
        pool = ctx.enter_context(tc.tile_pool(name="sbuf", bufs=1))
        psum = ctx.enter_context(tc.psum_pool(name="psum", bufs=1))

        def held(name, width, dtype, tag=None, bufs=1):
            return pool.tile([P, width], dtype, name=name, tag=tag or name, bufs=bufs, align_bytes=64)

        def bank(name, tag, bufs):
            return psum.tile([P, S], F32, name=name, tag=tag, bufs=bufs)

        picks = lists.tile([P, S // 16], U16, name="picks")
        places = lists.tile([P, S // 16], U16, name="places")
        nc.sync.dma_start(picks[:], offs)
        wgo_rows = held("wgo_rows", S, F32)
        nc.sync.dma_start(wgo_rows[:], wgo)
        ident = held("ident", P, F32)
        make_identity(nc, ident[:])

        tab_sc = held("tab_sc", K_PASSES * T, U8)
        wk_sc_raw = held("wk_sc_raw", K_PASSES * H, U8)
        wv_sc_raw = held("wv_sc_raw", N, U8)
        for plane in (tab_sc, wk_sc_raw, wv_sc_raw):
            nc.vector.memset(plane[:].bitcast(I32), 0)
        pages = [held("page0", T2, F32), held("page1", T2, F32)]
        for page in pages:
            nc.vector.memset(page[:], 0.0)

        def load_scale_rows(queue, plane, scales):
            for q in range(QUADS):
                queue.dma_start(
                    plane[32 * q : 32 * q + 4, :].bitcast(I32).rearrange("r (a w) -> r a w", a=K_PASSES),
                    scales[:, 4 * q : 4 * q + 4, :].bitcast(I32).rearrange("a r w -> r a w"),
                )

        tab = [held(f"tab{a}", T, I32, tag=f"pass_raw{a}") for a in range(K_PASSES)]
        wk_raw = held("wk_raw", K_PASSES * 2 * H, U8, tag="weight_raw")
        nc.sync.dma_start(tab[0][:], tab_words[0].rearrange("p t i -> p (t i)").bitcast(I32))
        load_scale_rows(nc.sync, tab_sc, tab_scales)
        nc.sync.dma_start(tab[1][:], tab_words[1].rearrange("p t i -> p (t i)").bitcast(I32))
        nc.sync.dma_start(
            wk_raw[:].bitcast(I32).rearrange("p (a w) -> p a w", a=K_PASSES),
            wk_words.bitcast(I32).rearrange("a p w -> p a w"),
        )
        load_scale_rows(nc.sync, wk_sc_raw, wk_scales)

        blocks = S // P
        wgo_turned = bank("wgo_turned", "short", 2)
        for n in range(blocks):
            nc.tensor.transpose(wgo_turned[:, n * P : (n + 1) * P], wgo_rows[:, n * P : (n + 1) * P], ident[:])
        gains = held("gains", PACK * S, F32)
        dealt = [held(f"wgo_dealt{t}", S, F32, tag=f"rows0{t}") for t in range(PACK)]
        for t in range(PACK):
            nc.scalar.copy(
                dealt[t][:].rearrange("j (n q r) -> j n q r", n=blocks, q=QUADS),
                wgo_turned[:]
                .rearrange("j (n r t) -> j t n r", n=blocks, t=PACK)[:, t]
                .unsqueeze(2)
                .broadcast_to([P, blocks, QUADS, P // QUADS]),
            )
        for t in range(PACK):
            acc = bank(f"gains{t}", "key", 4)
            for n in range(blocks):
                nc.tensor.transpose(acc[:, n * P : (n + 1) * P], dealt[t][:, n * P : (n + 1) * P], ident[:])
            nc.scalar.copy(gains[:, t * S : (t + 1) * S], acc[:])

        wk_codes = [held(f"wk_codes{b}", K_PASSES * 2 * PASS, U8) for b in range(H_PASSES)]
        wk_sc = [held(f"wk_sc{b}", K_PASSES * PASS, U8) for b in range(H_PASSES)]
        v_codes = [held(f"v_codes{a}", S, U32) for a in range(K_PASSES)]
        v_sc = [held(f"v_sc{a}", S, U8) for a in range(K_PASSES)]

        def deal_wk_codes(b):
            nc.scalar.copy(
                wk_codes[b][:].bitcast(U16).rearrange("p (a t q) -> p a q t", a=K_PASSES, t=PACK),
                wk_raw[:].bitcast(U16).rearrange("p (a b q t) -> p b a q t", a=K_PASSES, b=H_PASSES, t=PACK)[:, b],
            )

        def deal_wk_scales(b):
            nc.vector.tensor_copy(
                wk_sc[b][:].rearrange("p (a t q) -> p a q t", a=K_PASSES, t=PACK),
                wk_sc_raw[:].rearrange("p (a b q t) -> p b a q t", a=K_PASSES, b=H_PASSES, t=PACK)[:, b],
            )

        def tokens(h):
            return slice(h * HALF, (h + 1) * HALF)

        def entries(h):
            return slice(h * HALF // 16, (h + 1) * HALF // 16)

        def gather_codes(a, h):
            nc.vector.tensor_copy(v_codes[a][:, tokens(h)], tab[a][:].bitcast(U32).indirect(picks[:, entries(h)]))

        def gather_scales(a):
            nc.vector.tensor_copy(v_sc[a][:], tab_sc[:, a * T : (a + 1) * T].indirect(picks[:]))

        for b in range(H_PASSES):
            deal_wk_codes(b)
        nc.vector.tensor_copy(v_codes[0][:], tab[0][:].bitcast(U32).indirect(picks[:]))
        gather_scales(0)
        gather_scales(1)
        gather_codes(1, 0)
        deal_wk_scales(0)
        gather_codes(1, 1)
        deal_wk_scales(1)
        deal_wk_scales(2)

        wr_codes = {}
        wr_sc = {}
        wr_raw = {}
        wv_raw = {}
        wv_codes = {}

        def load_wr(a, g):
            wr_raw[a, g] = held(f"wr_raw{a}{g}", PACK * PASS, F32, tag=f"pass_raw{a}")
            nc.sync.dma_start(
                wr_raw[a, g][:].rearrange("p (j w) -> p j w", j=PACK),
                wr[a * PASS : (a + 1) * PASS, g * PASS : (g + 1) * PASS].rearrange("(p j) w -> p j w", j=PACK),
            )

        def quantize_wr(a, g, on_scalar):
            tag = f"wr_bf{a}" if g == 0 else ("relu_half1", "h_bf_last")[a]
            rounded = held(f"wr_bf{a}{g}", PACK * PASS, BF16, tag=tag)
            dst = rounded[:].rearrange("p (t m j) -> p m j t", t=PACK, j=PACK)
            src = wr_raw[a, g][:].rearrange("p (j m t) -> p m j t", j=PACK, t=PACK)
            if on_scalar:
                nc.scalar.copy(dst, src)
            else:
                nc.vector.tensor_copy(dst, src)
            wr_codes[a, g] = held(f"wr_codes{a}{g}", PASS, U32)
            wr_sc[a, g] = held(f"wr_sc{a}{g}", PASS, U8)
            nc.vector.quantize_mx(out=wr_codes[a, g][:].bitcast(FP8X4), scales=wr_sc[a, g][:], in_=rounded[:])

        def load_wv(g):
            wv_raw[g] = held(f"wv_raw{g}", H_PASSES * PASS, I32, tag="weight_raw" if g else "wv_raw0")
            nc.sync.dma_start(
                wv_raw[g][:].rearrange("p (b w) -> p b w", b=H_PASSES),
                wv_words[:, :, g * PASS : (g + 1) * PASS, :]
                .rearrange("b p n i -> b p (n i)")
                .bitcast(I32)
                .rearrange("b p w -> p b w"),
            )

        def deal_wv_codes(g, on_scalar):
            wv_codes[g] = held(f"wv_codes{g}", H_PASSES * PASS, I32, tag="h_bf_then_wv" if g else "wv_codes0")
            dst = wv_codes[g][:].rearrange("p (b t q) -> p b q t", b=H_PASSES, t=PACK)
            src = wv_raw[g][:].rearrange("p (b q t) -> p b q t", b=H_PASSES, t=PACK)
            if on_scalar:
                nc.scalar.copy(
                    wv_codes[g][:].bitcast(U32).rearrange("p (b t q) -> p b q t", b=H_PASSES, t=PACK),
                    wv_raw[g][:].bitcast(U32).rearrange("p (b q t) -> p b q t", b=H_PASSES, t=PACK),
                )
            else:
                nc.vector.tensor_copy(dst, src)

        load_wr(0, 0)
        for q in range(QUADS):
            nc.sync.dma_start(
                wv_sc_raw[32 * q : 32 * q + 4 * H_PASSES, :].bitcast(I32),
                wv_scales[:, 4 * q : 4 * q + 4, :].bitcast(I32),
            )
        load_wv(0)
        load_wr(1, 0)
        nc.sync.dma_start(places[:], offs2)

        h_codes = [held(f"h_codes{b}", S, U32) for b in range(H_PASSES)]
        h_sc = [held(f"h_sc{b}", S, U8) for b in range(H_PASSES)]

        def key_group(b, h, pairs_on_scalar):
            relu = held(f"relu{b}{h}", PACK * HALF, F32, tag=f"relu_half{h}", bufs=2 - h)
            for u in range(PAIRS):
                acc = bank(f"key{b}{h}{u}", "short", 2) if (b, h) == (0, 1) else bank(f"key{b}{h}{u}", "key", 4)
                for e in range(2):
                    for a in range(K_PASSES):
                        col = a * PASS + (2 * u + e) * P
                        nc.tensor.matmul_mx(
                            out=acc[:, e * HALF : (e + 1) * HALF],
                            lhsT=wk_codes[b][:, 2 * col : 2 * (col + P)].bitcast(FP4X4),
                            lhsT_scale=wk_sc[b][:, col : col + P],
                            rhs=v_codes[a][:, tokens(h)].bitcast(FP8X4),
                            rhs_scale=v_sc[a][:, tokens(h)],
                            start=(a == 0),
                            stop=(a == K_PASSES - 1),
                        )
                dst = relu[:, u * S : (u + 1) * S]
                if u < pairs_on_scalar:
                    nc.scalar.activation(dst, acc[:], ACT.Relu)
                else:
                    nc.vector.tensor_scalar_max(dst, acc[:], 0.0)
            return relu

        def square_group(b, h, relu):
            if (b, h) == (H_PASSES - 1, 1):
                h_bf = held(f"h_bf{b}{h}", PACK * HALF, BF16, tag="h_bf_last")
            elif (b, h) == (H_PASSES - 2, 1):
                h_bf = held(f"h_bf{b}{h}", PACK * HALF, BF16, tag="h_bf_then_wv")
            else:
                h_bf = held(f"h_bf{b}{h}", PACK * HALF, BF16, tag="h_bf", bufs=3)
            nc.scalar.activation(
                h_bf[:].rearrange("p (c i t) -> p c t i", t=PACK, i=4),
                relu[:].rearrange("p (t c i) -> p c t i", t=PACK, i=4),
                ACT.Square,
            )
            nc.vector.quantize_mx(
                out=h_codes[b][:, tokens(h)].bitcast(FP8X4), scales=h_sc[b][:, tokens(h)], in_=h_bf[:]
            )

        def rec_pass(acc, a, g, t, cols, start, stop):
            nc.tensor.matmul_mx(
                out=acc,
                lhsT=wr_codes[a, g][:, t * P : (t + 1) * P].bitcast(FP8X4),
                lhsT_scale=wr_sc[a, g][:, t * P : (t + 1) * P],
                rhs=v_codes[a][:, cols].bitcast(FP8X4),
                rhs_scale=v_sc[a][:, cols],
                start=start,
                stop=stop,
            )

        def val_pass(acc, b, g, t, cols, start, stop):
            col = b * PASS + t * P
            nc.tensor.matmul_mx(
                out=acc,
                lhsT=wv_codes[g][:, col : col + P].bitcast(FP8X4),
                lhsT_scale=wv_sc[4 * b :, g * PASS + t * P : g * PASS + (t + 1) * P],
                rhs=h_codes[b][:, cols].bitcast(FP8X4),
                rhs_scale=h_sc[b][:, cols],
                start=start,
                stop=stop,
            )

        steps = [[(0, 2 * u + e, h) for e in range(2)] for h in range(HALVES) for u in range(PAIRS)]
        steps = steps + [[(1, t, None)] for t in range(PACK)]
        gates = {}
        gated = {}

        def piece_cols(h):
            return slice(0, S) if h is None else tokens(h)

        def fill(acc, one_pass, passes, k):
            pieces = len(steps[k])
            width = S // pieces
            for n in range(passes):
                for e, (g, t, h) in enumerate(steps[k]):
                    first, final = (n, e) == (0, 0), (n, e) == (passes - 1, pieces - 1)
                    one_pass(acc[:, e * width : (e + 1) * width], n, g, t, piece_cols(h), first, final)

        def gate(k):
            acc = bank(f"rec{k}", "short", 2)
            fill(acc, rec_pass, K_PASSES, k)
            gates[k] = held(f"gate{k}", S, F32, tag=f"gate{k}")
            nc.scalar.activation(gates[k][:], acc[:], ACT.Sigmoid)

        def value(k):
            acc = bank(f"val{k}", "val", 2)
            fill(acc, val_pass, H_PASSES, k)
            if k == len(steps) - 1:
                gated[k] = held(f"gated{k}", S, F32, tag=f"woven{CHUNKS - 1}")
            elif k == 3:
                gated[k] = held(f"gated{k}", S, F32, tag="h_bf_last")
            else:
                gated[k] = held(f"gated{k}", S, F32, tag="gated", bufs=3)
            nc.vector.tensor_tensor(gated[k][:], acc[:], gates[k][:], ALU.mult)

        out_rows = out_0.rearrange("(g p t) m -> g t p m", t=PACK, p=P)

        def scatter(k):
            width = S // len(steps[k])
            for e, (g, t, h) in enumerate(steps[k]):
                offsets = places[:] if h is None else places[:, entries(h)]
                first = t * S + piece_cols(h).start
                nc.vector.tensor_tensor(
                    pages[t][:].indirect(offsets),
                    gated[k][:, e * width : (e + 1) * width],
                    gains[:, first : first + width],
                    ALU.mult,
                )
                if h != 0:
                    nc.sync.dma_start(out_rows[g, t], pages[t][:])

        last = N_GROUPS * PACK - 1
        rounded_rows = {}

        def round_page(i, c):
            g, t = divmod(i, PACK)
            if t == 0:
                rounded_rows[g, c] = held(f"rows{g}{c}", PACK * CHUNK, BF16, tag=f"rows{g}{c}")
            dst = rounded_rows[g, c][:, t * CHUNK : (t + 1) * CHUNK]
            src = pages[i % PAGES][:, c * CHUNK : (c + 1) * CHUNK]
            if i == last and c % 2 == 0:
                nc.vector.tensor_copy(dst, src)
            else:
                nc.scalar.copy(dst, src)

        y_sc = {}

        def planes(g, c):
            woven = held(f"woven{g}{c}", PACK * CHUNK, BF16, tag=f"woven{c}")
            dst = woven[:].rearrange("p (c i t) -> p c t i", t=PACK, i=4)
            src = rounded_rows[g, c][:].rearrange("p (t c i) -> p c t i", t=PACK, i=4)
            if (g == N_GROUPS - 1 and c % 2 == 0) or (g, c) == (0, 0):
                nc.vector.tensor_copy(dst, src)
            else:
                nc.scalar.copy(dst, src)
            if c == 0:
                y_sc[g] = held(f"y_sc{g}", T2, U8)
            codes = held(f"y_codes{g}{c}", CHUNK, I32, tag="y_codes", bufs=4)
            nc.vector.quantize_mx(out=codes[:].bitcast(FP8X4), scales=y_sc[g][:, c * CHUNK : (c + 1) * CHUNK], in_=woven[:])
            nc.sync.dma_start(
                out_1[g].rearrange("p m t -> p (m t)").bitcast(I32)[:, c * CHUNK : (c + 1) * CHUNK], codes[:]
            )

        def store_scales(g, queue):
            for q in range(QUADS):
                queue.dma_start(
                    out_2[g, 4 * q : 4 * q + 4, :].bitcast(I32),
                    y_sc[g][32 * q : 32 * q + 4, :].bitcast(I32),
                )

        def round_whole_page(i):
            for c in range(CHUNKS):
                round_page(i, c)

        wv_sc = held("wv_sc", N, U8)

        relu = key_group(0, 0, 2)
        quantize_wr(0, 0, False)
        square_group(0, 0, relu)
        deal_wv_codes(0, False)
        nc.vector.tensor_copy(
            wv_sc[:].rearrange("p (g t q) -> p g q t", g=N_GROUPS, t=PACK),
            wv_sc_raw[:].rearrange("p (g q t) -> p g q t", g=N_GROUPS, t=PACK),
        )
        load_wr(0, 1)
        relu = key_group(1, 0, 2)
        quantize_wr(1, 0, False)
        load_wr(1, 1)
        load_wv(1)
        square_group(1, 0, relu)
        square_group(2, 0, key_group(2, 0, 2))
        gate(0)
        value(0)
        pages.append(held("page2", T2, F32, tag="gate0"))
        nc.gpsimd.memset(pages[2][:], 0.0)
        gate(1)
        scatter(0)
        value(1)
        pages.append(held("page3", T2, F32, tag="gate1"))
        nc.gpsimd.memset(pages[3][:], 0.0)
        for b in range(H_PASSES):
            square_group(b, 1, key_group(b, 1, 2))
        scatter(1)
        gate(2)
        gate(3)
        value(2)
        scatter(2)
        quantize_wr(0, 1, True)
        quantize_wr(1, 1, True)
        deal_wv_codes(1, False)
        value(3)
        scatter(3)
        round_whole_page(0)
        gate(4)
        value(4)
        gate(5)
        value(5)
        round_whole_page(1)
        scatter(4)
        gate(6)
        value(6)
        round_whole_page(2)
        scatter(5)
        gate(7)
        round_whole_page(3)
        scatter(6)
        for c in range(CHUNKS):
            planes(0, c)
        store_scales(0, nc.sync)
        value(7)
        for i in range(PACK, last):
            round_whole_page(i)
        scatter(7)
        for c in range(CHUNKS):
            round_page(last, c)
            planes(1, c)
        store_scales(1, nc.scalar)
